import numpy as np
import ml_dtypes


def mxq(x, axis, fmt="e4m3"):
    dtype, down = {"e4m3": (ml_dtypes.float8_e4m3fn, 7), "e5m2": (ml_dtypes.float8_e5m2, 14)}[fmt]
    v = np.moveaxis(np.asarray(x, np.float32).astype(ml_dtypes.bfloat16).astype(np.float64), axis, -1)
    blocks = v.reshape(v.shape[:-1] + (-1, 32))
    amax = np.abs(blocks).max(-1, keepdims=True)
    byte = np.maximum(np.where(amax > 0, np.frexp(amax)[1] - 1 + 127, 0) - down, 1)
    scale = np.exp2(byte - 127.0)
    codes = (blocks / scale).astype(np.float32).astype(dtype).astype(np.float64)
    return np.moveaxis((codes * scale).reshape(v.shape), -1, axis)


WIDE = False


def mx_kscale(k):
    if not WIDE:
        return np.ones(k)
    levels = np.array([10, -10, 5, -5, 0])
    if k % 512:
        return np.exp2(np.random.permutation(np.resize(levels, k // 32))).repeat(32)
    a = np.empty((k // 512, 16))
    for p in range(k // 512):
        a[p, :8] = np.random.permutation(np.resize(levels, 8))
        for g in range(8):
            far = levels[np.abs(levels - a[p, g]) >= 10]
            a[p, g + 8] = far[np.random.randint(len(far))]
    return np.exp2(a.ravel()).repeat(32)


def f64(x):
    return np.asarray(x).astype(np.float64)


def striped(idx):
    return np.tile(idx.reshape(-1, 16).T, (8, 1)).astype(np.uint16)


def unstriped(offs):
    return offs[:16].T.reshape(-1).astype(np.int64)


def striped8(idx):
    return np.concatenate([x.reshape(-1, 16).T for x in idx]).astype(np.uint16)


def runs(offs, k):
    lists = np.stack([offs[16 * r : 16 * r + 16].T.reshape(-1) for r in range(8)]).astype(np.int64)
    return lists[np.arange(k) % 512 // 64]


def pack_weight(w):
    k, n = w.shape
    w = f64(np.asarray(w, np.float32).astype(ml_dtypes.bfloat16)).reshape(k // 32, 32, n)
    amax = np.abs(w).max(1)
    byte = np.clip(np.where(amax > 0, np.frexp(amax)[1] - 1 + 127 - 7, 1), 1, 254)
    scaled = (w * np.exp2(127.0 - byte)[:, None, :]).reshape(k, n).astype(np.float32)
    words = np.ascontiguousarray(scaled.reshape(k // 512, 128, 4, n).transpose(0, 1, 3, 2)).astype(ml_dtypes.float8_e4m3fn).view(np.uint8)
    return words, np.ascontiguousarray(byte.astype(np.uint8).reshape(k // 512, 16, n))


def unpack_weight(words, scales):
    g, p, n, _ = words.shape
    vals = np.ascontiguousarray(words).view(ml_dtypes.float8_e4m3fn).astype(np.float64) * np.repeat(np.exp2(scales.astype(np.float64) - 127.0), 8, axis=1)[..., None]
    return vals.transpose(0, 1, 3, 2).reshape(g * 512, n)


E2M1 = np.array([0.0, 0.5, 1.0, 1.5, 2.0, 3.0, 4.0, 6.0, -0.0, -0.5, -1.0, -1.5, -2.0, -3.0, -4.0, -6.0])


def pack_fp4(w):
    k, n = w.shape
    w = f64(np.asarray(w, np.float32).astype(ml_dtypes.bfloat16)).reshape(k // 32, 32, n)
    amax = np.abs(w).max(1)
    mant, ex = np.frexp(amax / 6.0)
    byte = np.clip(np.where(amax > 0, np.where(mant > 0.5, ex, ex - 1) + 127, 1), 1, 254)
    scaled = (w * np.exp2(127.0 - byte)[:, None, :]).reshape(k, n).astype(np.float32)
    c = np.ascontiguousarray(scaled.reshape(k // 512, 128, 4, n).transpose(0, 1, 3, 2)).astype(ml_dtypes.float4_e2m1fn).view(np.uint8) & 0xF
    words = (c[..., 0::2] | (c[..., 1::2] << 4)).reshape(k // 512, 128, 2 * n)
    return np.ascontiguousarray(words), np.ascontiguousarray(byte.astype(np.uint8).reshape(k // 512, 16, n))


def unpack_fp4(words, scales):
    g, _, n = scales.shape
    words = np.ascontiguousarray(words).reshape(g, 128, n, 2)
    nib = np.empty((g, 128, n, 4), np.uint8)
    nib[..., 0::2] = words & 0xF
    nib[..., 1::2] = words >> 4
    vals = E2M1[nib] * np.repeat(np.exp2(scales.astype(np.float64) - 127.0), 8, axis=1)[..., None]
    return vals.transpose(0, 1, 3, 2).reshape(g * 512, n)


K, T, S, N, G, H, W = 512, 1024, 512, 512, 2048, 512, 256


def setup_inputs():
    n = np.random.standard_normal
    s = mx_kscale(K)[:, None]
    u = mx_kscale(S)
    packed_xT = pack_weight(n((K, T)) * s)
    packed_dT = pack_weight(n((K, G)) / s)
    packed_w1 = pack_fp4(n((H, N)) / np.sqrt(2 * H) / u[:, None])
    packed_w2 = pack_fp4(n((K, N)) / np.sqrt(2 * K) / s)
    perm = np.random.permutation(S)
    perm2 = np.random.permutation(S)
    return {
        "x_words": packed_xT[0],
        "x_scales": packed_xT[1],
        "d_words": packed_dT[0],
        "d_scales": packed_dT[1],
        "gn": (np.random.uniform(0.5, 1.5, (H, 1)) * u[:, None]).astype(np.float32),
        "w1_words": packed_w1[0],
        "w1_scales": packed_w1[1],
        "w2_words": packed_w2[0],
        "w2_scales": packed_w2[1],
        "offs": striped(np.random.permutation(T)[:S]),
        "k1": striped8(np.random.randint(0, G, (8, H))),
        "hz": striped8(np.random.randint(0, T, (8, S))),
        "k2": striped8(np.random.randint(0, G, (8, H))),
        "n1": striped(np.random.permutation(S)),
        "n2": striped(np.random.permutation(S)),
        "two": striped(np.random.permutation(T)[:S]),
        "n3": striped(perm[:W]),
        "n4": striped(perm[W:]),
        "n5": striped(perm2[:W]),
        "n6": striped(perm2[W:]),
        "n7": striped(np.random.permutation(S)),
    }


def reference(x_words, x_scales, d_words, d_scales, gn, w1_words, w1_scales, w2_words, w2_scales, offs, k1, hz, k2, n1, n2, two, n3, n4, n5, n6, n7):
    d_k1 = unpack_weight(d_words, d_scales)[np.arange(K)[:, None], runs(k1, K)]
    xq = unpack_weight(x_words, x_scales)[:, unstriped(offs)]
    d_k2 = unpack_weight(d_words, d_scales)[np.arange(K)[:, None], runs(k2, K)]
    x_hz = unpack_weight(x_words, x_scales)[np.arange(K)[:, None], runs(hz, K)]
    h = 0.0625 * (d_k1.T @ xq + d_k2.T @ x_hz)
    ds = np.zeros((H, S))
    ds[:, unstriped(n1)] = h
    ds2 = np.zeros((H, S))
    ds2[:, unstriped(n2)] = h
    z = f64(gn) * (ds - ds2)
    x_two = unpack_weight(x_words, x_scales)[:, unstriped(two)]
    h2 = unpack_fp4(w1_words, w1_scales).T @ mxq(z, 0, "e4m3") + unpack_fp4(w2_words, w2_scales).T @ x_two
    pa = h2[:, unstriped(n3)]
    pb = h2[:, unstriped(n4)]
    ra = pb - pa
    ua = np.zeros((N, S))
    ua[:, unstriped(n5)] = ra
    ub = ua.copy()
    ub[:, unstriped(n6)] = pa
    return np.maximum(ub, h2[:, unstriped(n7)])

@@ -1,0 +1,211 @@
+from contextlib import ExitStack
+
+import concourse.mybir as mybir
+
+K, T, S, N, G, H, W = 512, 1024, 512, 512, 2048, 512, 256
+FLOPS = 2 * (2 * K * H * S + H * N * S + K * N * S)
+
+F32 = mybir.dt.float32
+BF16 = mybir.dt.bfloat16
+I32 = mybir.dt.int32
+U32 = mybir.dt.uint32
+U16 = mybir.dt.uint16
+U8 = mybir.dt.uint8
+FP8X4 = mybir.dt.float8_e4m3fn_x4
+FP4X4 = mybir.dt.float4_e2m1fn_x4
+COPY = mybir.ActivationFunctionType.Copy
+ALU = mybir.AluOpType
+
+P = 128
+PACK = 4
+STRIPE = 16
+FIRST = 128
+REST = S - FIRST
+
+
+def tile_picked_mthzntsndsubcphw_none_p_kernel(
+    tc, x_words, x_scales, d_words, d_scales, gn, w1_words, w1_scales, w2_words, w2_scales,
+    offs, k1, hz, k2, n1, n2, two, n3, n4, n5, n6, n7, out,
+):
+    nc = tc.nc
+    with ExitStack() as ctx:
+        lists = ctx.enter_context(tc.tile_pool(name="lists", bufs=1))
+        keep = ctx.enter_context(tc.tile_pool(name="keep", bufs=1))
+        reuse = ctx.enter_context(tc.tile_pool(name="reuse", bufs=1))
+        psum = ctx.enter_context(tc.psum_pool(name="psum", bufs=1))
+
+        def load_list(ap, name):
+            t = lists.tile([P, ap.shape[1]], U16, name=name)
+            nc.sync.dma_start(t[:], ap)
+            return t
+
+        def entries(lst, lo, hi):
+            return lst[:, lo // STRIPE : hi // STRIPE]
+
+        def load_scale_table(ap, cols, name):
+            t = keep.tile([P, cols], U8, name=name, align_bytes=64)
+            rows = ap[0].bitcast(I32)
+            nc.scalar.dma_start(t[:].bitcast(I32), rows.unsqueeze(1).to_broadcast([16, 8, cols // 4]))
+            return t
+
+        def load_word_table(ap, cols, name):
+            t = keep.tile([P, cols], I32, name=name, align_bytes=64)
+            nc.sync.dma_start(t[:], ap[0].rearrange("p n t -> p (n t)").bitcast(I32))
+            return t
+
+        def place_scale_rows(dst, src, queues):
+            for a in range(4):
+                q = queues[a % len(queues)]
+                q.dma_start(dst[a:P:32, :].bitcast(I32), src[8 * a : P : 32, :].bitcast(I32))
+
+        d_sc = load_scale_table(d_scales, G, "d_sc")
+        k1_l = load_list(k1, "k1_l")
+        k2_l = load_list(k2, "k2_l")
+        x_sc = load_scale_table(x_scales, T, "x_sc")
+        offs_l = load_list(offs, "offs_l")
+        hz_l = load_list(hz, "hz_l")
+        d_w = load_word_table(d_words, G, "d_w")
+        x_w = load_word_table(x_words, T, "x_w")
+        gain_raw = keep.tile([P, PACK], F32, name="gain_raw")
+        nc.sync.dma_start(gain_raw[:], gn.rearrange("(p t) o -> p (t o)", t=PACK))
+        n1_l = load_list(n1, "n1_l")
+        n2_l = load_list(n2, "n2_l")
+        gain = keep.tile([P, PACK], F32, name="gain")
+        nc.scalar.activation(gain[:], gain_raw[:], COPY, scale=0.0625)
+
+        def gather(dst, table, dtype, lst, lo, hi):
+            nc.vector.tensor_copy(dst, table[:].bitcast(dtype).indirect(entries(lst, lo, hi)) if dtype is U32 else table[:].indirect(entries(lst, lo, hi)))
+
+        placed1 = keep.tile([P, 2 * H + 2 * FIRST], U8, name="placed1", align_bytes=64)
+        placed2 = keep.tile([P, 2 * REST], U8, name="placed2", align_bytes=64)
+        placed3 = keep.tile([P, S], U8, name="placed3", align_bytes=64)
+        nc.gpsimd.memset(placed1[:].bitcast(I32), 0)
+        nc.gpsimd.memset(placed2[:].bitcast(I32), 0)
+        nc.gpsimd.memset(placed3[:].bitcast(I32), 0)
+
+        picked = reuse.tile([P, 2 * H + 2 * FIRST], U8, name="picked", align_bytes=64, offset=0)
+        gather(picked[:, 0:H], d_sc, U8, k1_l, 0, H)
+        gather(picked[:, H : 2 * H], d_sc, U8, k2_l, 0, H)
+        gather(picked[:, 2 * H : 2 * H + FIRST], x_sc, U8, offs_l, 0, FIRST)
+        gather(picked[:, 2 * H + FIRST :], x_sc, U8, hz_l, 0, FIRST)
+        place_scale_rows(placed1, picked, (nc.sync, nc.scalar))
+
+        code_w = keep.tile([P, 2 * H], U32, name="code_w", align_bytes=64)
+        gather(code_w[:, 0:H], d_w, U32, k1_l, 0, H)
+        gather(code_w[:, H:], d_w, U32, k2_l, 0, H)
+        tok_first = keep.tile([P, 2, FIRST], U32, name="tok_first", align_bytes=64)
+        gather(tok_first[:, 0, :], x_w, U32, offs_l, 0, FIRST)
+        gather(tok_first[:, 1, :], x_w, U32, hz_l, 0, FIRST)
+
+        ds = [keep.tile([P, S], F32, name="ds%d" % t) for t in range(PACK)]
+        ds2 = [keep.tile([P, S], F32, name="ds2_%d" % t) for t in range(PACK)]
+        dealt_first = keep.tile([P, 2, P], U32, name="dealt_first", align_bytes=64)
+        dealt_later = reuse.tile([P, PACK - 1, 2, P], U32, name="dealt_later", align_bytes=64, offset=2 * REST)
+        dealt_w = [dealt_first[:]] + [dealt_later[:, t] for t in range(PACK - 1)]
+        picked_rest = reuse.tile([P, 2 * REST], U8, name="picked_rest", align_bytes=64, offset=0)
+        dealt_s = [keep.tile([P, 2, P], U8, name="dealt_s%d" % t, align_bytes=64) for t in range(PACK)]
+
+        def first_product(t, bank, tok, tok_scale, lo, hi, base):
+            for c in range(2):
+                nc.tensor.matmul_mx(
+                    out=bank[:, lo - base : hi - base],
+                    lhsT=dealt_w[t][:, c, :].bitcast(FP8X4),
+                    lhsT_scale=dealt_s[t][:, c, :],
+                    rhs=tok[:, c, lo - base : hi - base].bitcast(FP8X4),
+                    rhs_scale=tok_scale[:, c, lo - base : hi - base],
+                    start=(c == 0),
+                    stop=(c == 1),
+                )
+
+        def scatter_h(t, bank, lo, hi):
+            h = keep.tile([P, hi - lo], F32, name="h%d_%d" % (t, lo))
+            nc.vector.tensor_scalar(h[:], bank[:, 0 : hi - lo], gain[:, t : t + 1], None, ALU.mult)
+            nc.scalar.activation(ds[t][:].indirect(entries(n1_l, lo, hi)), h[:], COPY)
+            nc.scalar.activation(ds2[t][:].indirect(entries(n2_l, lo, hi)), h[:], COPY)
+
+        first_scale = placed1[:, 2 * H :].rearrange("p (c n) -> p c n", c=2)
+        for t in range(PACK):
+            nc.vector.tensor_copy(
+                dealt_w[t].bitcast(I32),
+                code_w[:].bitcast(I32).rearrange("p (c m t) -> p t c m", c=2, t=PACK)[:, t],
+            )
+            nc.vector.tensor_copy(
+                dealt_s[t][:], placed1[:, 0 : 2 * H].rearrange("p (c m t) -> p t c m", c=2, t=PACK)[:, t]
+            )
+            bank = psum.tile([P, FIRST], F32, name="bank_first", bufs=2)
+            first_product(t, bank, tok_first, first_scale, 0, FIRST, 0)
+            scatter_h(t, bank, 0, FIRST)
+            if t == 1:
+                gather(picked_rest[:, 0:REST], x_sc, U8, offs_l, FIRST, S)
+                gather(picked_rest[:, REST:], x_sc, U8, hz_l, FIRST, S)
+                place_scale_rows(placed2, picked_rest, (nc.sync,))
+
+        tok_rest = keep.tile([P, 2, REST], U32, name="tok_rest", tag="code_w", align_bytes=64)
+        gather(tok_rest[:, 0, :], x_w, U32, offs_l, FIRST, S)
+        gather(tok_rest[:, 1, :], x_w, U32, hz_l, FIRST, S)
+        rest_scale = placed2[:].rearrange("p (c n) -> p c n", c=2)
+
+        two_l = load_list(two, "two_l")
+        n3_l = load_list(n3, "n3_l")
+        n4_l = load_list(n4, "n4_l")
+        n5_l = load_list(n5, "n5_l")
+        n6_l = load_list(n6, "n6_l")
+        n7_l = load_list(n7, "n7_l")
+        w_codes = keep.tile([P, 2, 2 * N], U8, name="w_codes", tag="d_w", align_bytes=64)
+        w_sc = keep.tile([P, 2, N], U8, name="w_sc", tag="placed1", align_bytes=64)
+        nc.gpsimd.memset(w_sc[:].rearrange("p a n -> p (a n)").bitcast(I32), 0)
+        for c, (words, scales) in enumerate(((w1_words, w1_scales), (w2_words, w2_scales))):
+            nc.sync.dma_start(w_codes[:, c, :].bitcast(I32), words[0].bitcast(I32))
+            for a in range(4):
+                nc.sync.dma_start(w_sc[a:P:32, c, :].bitcast(I32), scales[0, a:16:4, :].bitcast(I32))
+
+        z = keep.tile([P, S, PACK], BF16, name="z", align_bytes=64)
+        for t in range(PACK):
+            bank = psum.tile([P, REST], F32, name="bank_rest", bufs=2)
+            first_product(t, bank, tok_rest, rest_scale, FIRST, FIRST + 256, FIRST)
+            first_product(t, bank, tok_rest, rest_scale, FIRST + 256, S, FIRST)
+            scatter_h(t, bank, FIRST, S)
+            nc.vector.tensor_tensor(z[:, :, t], ds[t][:], ds2[t][:], ALU.subtract)
+            if t == 0:
+                picked_two = reuse.tile([P, S], U8, name="picked_two", align_bytes=64, offset=0)
+                gather(picked_two[:], x_sc, U8, two_l, 0, S)
+                place_scale_rows(placed3, picked_two, (nc.sync,))
+                two_w = keep.tile([P, S], U32, name="two_w", tag="tok_first", align_bytes=64)
+                gather(two_w[:], x_w, U32, two_l, 0, S)
+
+        def second_product(b, bank, c, rhs, rhs_scale):
+            nc.tensor.matmul_mx(
+                out=bank[:],
+                lhsT=w_codes[:, c, 2 * P * b : 2 * P * (b + 1)].bitcast(FP4X4),
+                lhsT_scale=w_sc[:, c, P * b : P * (b + 1)],
+                rhs=rhs[:].bitcast(FP8X4),
+                rhs_scale=rhs_scale[:],
+                start=(c == 1),
+                stop=(c == 0),
+            )
+
+        banks = [psum.tile([P, S], F32, name="bank_out%d" % b) for b in range(N // P)]
+        for b in range(N // P):
+            second_product(b, banks[b], 1, two_w, placed3)
+
+        z_codes = keep.tile([P, S], U32, name="z_codes", align_bytes=64)
+        z_scales = keep.tile([P, S], U8, name="z_scales", align_bytes=64)
+        nc.vector.quantize_mx(out=z_codes[:].bitcast(FP8X4), scales=z_scales[:], in_=z[:].rearrange("p n t -> p (n t)"))
+
+        for b in range(N // P):
+            second_product(b, banks[b], 0, z_codes, z_scales)
+            h2 = keep.tile([P, S], F32, name="h2_%d" % b)
+            nc.vector.tensor_copy(h2[:], banks[b][:])
+            pa = keep.tile([P, W], F32, name="pa%d" % b)
+            nc.scalar.activation(pa[:], h2[:].indirect(n3_l[:]), COPY)
+            ra = keep.tile([P, W], F32, name="ra%d" % b)
+            nc.vector.tensor_tensor(ra[:], h2[:].indirect(n4_l[:]), pa[:], ALU.subtract)
+            ub = keep.tile([P, S], F32, name="ub%d" % b)
+            nc.scalar.activation(ub[:].indirect(n6_l[:]), pa[:], COPY)
+            nc.scalar.activation(ub[:].indirect(n5_l[:]), ra[:], COPY)
+            other = keep.tile([P, S], F32, name="other%d" % b, tag="ra%d" % b)
+            for lo, hi in ((0, REST), (REST, S)):
+                nc.scalar.activation(other[:, lo:hi], h2[:].indirect(entries(n7_l, lo, hi)), COPY)
+                res = keep.tile([P, hi - lo], F32, name="res%d_%d" % (b, lo))
+                nc.vector.tensor_tensor(res[:], ub[:, lo:hi], other[:, lo:hi], ALU.max)
+                nc.sync.dma_start(out[P * b : P * (b + 1), lo:hi], res[:])

@@ -50,7 +50,7 @@ def tile_picked_mthzntsndsubcphw_none_p_kernel(
 
         def load_word_table(ap, cols, name):
             t = keep.tile([P, cols], I32, name=name, align_bytes=64)
-            nc.sync.dma_start(t[:], ap[0].rearrange("p n t -> p (n t)").bitcast(I32))
+            nc.gpsimd.dma_start(t[:], ap[0].rearrange("p n t -> p (n t)").bitcast(I32))
             return t
 
         def place_scale_rows(dst, src, queues):
@@ -58,12 +58,12 @@ def tile_picked_mthzntsndsubcphw_none_p_kernel(
                 q = queues[a % len(queues)]
                 q.dma_start(dst[a:P:32, :].bitcast(I32), src[8 * a : P : 32, :].bitcast(I32))
 
-        d_sc = load_scale_table(d_scales, G, "d_sc")
-        k1_l = load_list(k1, "k1_l")
-        k2_l = load_list(k2, "k2_l")
         x_sc = load_scale_table(x_scales, T, "x_sc")
         offs_l = load_list(offs, "offs_l")
         hz_l = load_list(hz, "hz_l")
+        d_sc = load_scale_table(d_scales, G, "d_sc")
+        k1_l = load_list(k1, "k1_l")
+        k2_l = load_list(k2, "k2_l")
         d_w = load_word_table(d_words, G, "d_w")
         x_w = load_word_table(x_words, T, "x_w")
         gain_raw = keep.tile([P, PACK], F32, name="gain_raw")
@@ -79,18 +79,18 @@ def tile_picked_mthzntsndsubcphw_none_p_kernel(
         placed1 = keep.tile([P, 2 * H + 2 * FIRST], U8, name="placed1", align_bytes=64)
         placed2 = keep.tile([P, 2 * REST], U8, name="placed2", align_bytes=64)
         placed3 = keep.tile([P, S], U8, name="placed3", align_bytes=64)
-        nc.gpsimd.memset(placed1[:].bitcast(I32), 0)
-        nc.gpsimd.memset(placed2[:].bitcast(I32), 0)
-        nc.gpsimd.memset(placed3[:].bitcast(I32), 0)
+        nc.vector.memset(placed1[:].bitcast(I32), 0)
+        nc.vector.memset(placed2[:].bitcast(I32), 0)
+        nc.vector.memset(placed3[:].bitcast(I32), 0)
 
         picked = reuse.tile([P, 2 * H + 2 * FIRST], U8, name="picked", align_bytes=64, offset=0)
-        gather(picked[:, 0:H], d_sc, U8, k1_l, 0, H)
-        gather(picked[:, H : 2 * H], d_sc, U8, k2_l, 0, H)
         gather(picked[:, 2 * H : 2 * H + FIRST], x_sc, U8, offs_l, 0, FIRST)
         gather(picked[:, 2 * H + FIRST :], x_sc, U8, hz_l, 0, FIRST)
+        gather(picked[:, 0:H], d_sc, U8, k1_l, 0, H)
+        gather(picked[:, H : 2 * H], d_sc, U8, k2_l, 0, H)
         place_scale_rows(placed1, picked, (nc.sync, nc.scalar))
 
-        code_w = keep.tile([P, 2 * H], U32, name="code_w", align_bytes=64)
+        code_w = reuse.tile([P, 2 * H], U32, name="code_w", align_bytes=64, offset=4096)
         gather(code_w[:, 0:H], d_w, U32, k1_l, 0, H)
         gather(code_w[:, H:], d_w, U32, k2_l, 0, H)
         tok_first = keep.tile([P, 2, FIRST], U32, name="tok_first", align_bytes=64)
@@ -100,9 +100,8 @@ def tile_picked_mthzntsndsubcphw_none_p_kernel(
         ds = [keep.tile([P, S], F32, name="ds%d" % t) for t in range(PACK)]
         ds2 = [keep.tile([P, S], F32, name="ds2_%d" % t) for t in range(PACK)]
         dealt_first = keep.tile([P, 2, P], U32, name="dealt_first", align_bytes=64)
-        dealt_later = reuse.tile([P, PACK - 1, 2, P], U32, name="dealt_later", align_bytes=64, offset=2 * REST)
+        dealt_later = reuse.tile([P, PACK - 1, 2, P], U32, name="dealt_later", align_bytes=64, offset=0)
         dealt_w = [dealt_first[:]] + [dealt_later[:, t] for t in range(PACK - 1)]
-        picked_rest = reuse.tile([P, 2 * REST], U8, name="picked_rest", align_bytes=64, offset=0)
         dealt_s = [keep.tile([P, 2, P], U8, name="dealt_s%d" % t, align_bytes=64) for t in range(PACK)]
 
         def first_product(t, bank, tok, tok_scale, lo, hi, base):
@@ -132,15 +131,16 @@ def tile_picked_mthzntsndsubcphw_none_p_kernel(
             nc.vector.tensor_copy(
                 dealt_s[t][:], placed1[:, 0 : 2 * H].rearrange("p (c m t) -> p t c m", c=2, t=PACK)[:, t]
             )
-            bank = psum.tile([P, FIRST], F32, name="bank_first", bufs=2)
+            bank = psum.tile([P, FIRST], F32, name="bank_first%d" % t, tag="bank_out%d" % t)
             first_product(t, bank, tok_first, first_scale, 0, FIRST, 0)
             scatter_h(t, bank, 0, FIRST)
-            if t == 1:
-                gather(picked_rest[:, 0:REST], x_sc, U8, offs_l, FIRST, S)
-                gather(picked_rest[:, REST:], x_sc, U8, hz_l, FIRST, S)
-                place_scale_rows(placed2, picked_rest, (nc.sync,))
 
-        tok_rest = keep.tile([P, 2, REST], U32, name="tok_rest", tag="code_w", align_bytes=64)
+        picked_rest = reuse.tile([P, 2 * REST], U8, name="picked_rest", align_bytes=64, offset=4096 + 8 * REST)
+        gather(picked_rest[:, 0:REST], x_sc, U8, offs_l, FIRST, S)
+        gather(picked_rest[:, REST:], x_sc, U8, hz_l, FIRST, S)
+        place_scale_rows(placed2, picked_rest, (nc.sync,))
+
+        tok_rest = reuse.tile([P, 2, REST], U32, name="tok_rest", align_bytes=64, offset=4096)
         gather(tok_rest[:, 0, :], x_w, U32, offs_l, FIRST, S)
         gather(tok_rest[:, 1, :], x_w, U32, hz_l, FIRST, S)
         rest_scale = placed2[:].rearrange("p (c n) -> p c n", c=2)
@@ -165,37 +165,56 @@ def tile_picked_mthzntsndsubcphw_none_p_kernel(
             first_product(t, bank, tok_rest, rest_scale, FIRST, FIRST + 256, FIRST)
             first_product(t, bank, tok_rest, rest_scale, FIRST + 256, S, FIRST)
             scatter_h(t, bank, FIRST, S)
-            nc.vector.tensor_tensor(z[:, :, t], ds[t][:], ds2[t][:], ALU.subtract)
-            if t == 0:
-                picked_two = reuse.tile([P, S], U8, name="picked_two", align_bytes=64, offset=0)
-                gather(picked_two[:], x_sc, U8, two_l, 0, S)
-                place_scale_rows(placed3, picked_two, (nc.sync,))
-                two_w = keep.tile([P, S], U32, name="two_w", tag="tok_first", align_bytes=64)
-                gather(two_w[:], x_w, U32, two_l, 0, S)
+            if t < PACK - 1:
+                nc.vector.tensor_tensor(z[:, :, t], ds[t][:], ds2[t][:], ALU.subtract)
 
-        def second_product(b, bank, c, rhs, rhs_scale):
+        picked_two = reuse.tile([P, S], U8, name="picked_two", align_bytes=64, offset=0)
+        gather(picked_two[:], x_sc, U8, two_l, 0, S)
+        place_scale_rows(placed3, picked_two, (nc.sync,))
+        two_w = reuse.tile([P, S], U32, name="two_w", align_bytes=64, offset=4096)
+        gather(two_w[:], x_w, U32, two_l, 0, S)
+
+        def second_product(b, bank, c, rhs, rhs_scale, lo, hi):
             nc.tensor.matmul_mx(
                 out=bank[:],
                 lhsT=w_codes[:, c, 2 * P * b : 2 * P * (b + 1)].bitcast(FP4X4),
                 lhsT_scale=w_sc[:, c, P * b : P * (b + 1)],
-                rhs=rhs[:].bitcast(FP8X4),
-                rhs_scale=rhs_scale[:],
+                rhs=rhs[:, lo:hi].bitcast(FP8X4),
+                rhs_scale=rhs_scale[:, lo:hi],
                 start=(c == 1),
                 stop=(c == 0),
             )
 
-        banks = [psum.tile([P, S], F32, name="bank_out%d" % b) for b in range(N // P)]
-        for b in range(N // P):
-            second_product(b, banks[b], 1, two_w, placed3)
+        parts = [(0, W, S), (0, 0, W)] + [(b, 0, S) for b in range(1, N // P)]
+        banks = [psum.tile([P, hi - lo], F32, name="bank_out%d" % i) for i, (b, lo, hi) in enumerate(parts)]
+        for bank, (b, lo, hi) in zip(banks, parts):
+            second_product(b, bank, 1, two_w, placed3, lo, hi)
 
+        last = PACK - 1
+        z_last = keep.tile([P, S], BF16, name="z_last")
+        nc.vector.tensor_tensor(z_last[:, 0:W], ds[last][:, 0:W], ds2[last][:, 0:W], ALU.subtract)
+        nc.vector.tensor_tensor(z_last[:, W:S], ds[last][:, W:S], ds2[last][:, W:S], ALU.subtract)
+        nc.scalar.copy(z[:, 0:W, last], z_last[:, 0:W])
+        nc.vector.tensor_copy(z[:, W:S, last], z_last[:, W:S])
         z_codes = keep.tile([P, S], U32, name="z_codes", align_bytes=64)
         z_scales = keep.tile([P, S], U8, name="z_scales", align_bytes=64)
-        nc.vector.quantize_mx(out=z_codes[:].bitcast(FP8X4), scales=z_scales[:], in_=z[:].rearrange("p n t -> p (n t)"))
+        for lo, hi in ((W, S), (0, W)):
+            nc.vector.quantize_mx(
+                out=z_codes[:, lo:hi].bitcast(FP8X4),
+                scales=z_scales[:, lo:hi],
+                in_=z[:, lo:hi, :].rearrange("p n t -> p (n t)"),
+            )
+
+        h2s = [keep.tile([P, S], F32, name="h2_%d" % b) for b in range(N // P)]
+        for bank, (b, lo, hi) in zip(banks, parts):
+            second_product(b, bank, 0, z_codes, z_scales, lo, hi)
+            if b == 0:
+                nc.scalar.copy(h2s[b][:, lo:hi], bank[:])
 
         for b in range(N // P):
-            second_product(b, banks[b], 0, z_codes, z_scales)
-            h2 = keep.tile([P, S], F32, name="h2_%d" % b)
-            nc.vector.tensor_copy(h2[:], banks[b][:])
+            h2 = h2s[b]
+            if b > 0:
+                nc.vector.tensor_copy(h2[:], banks[b + 1][:])
             pa = keep.tile([P, W], F32, name="pa%d" % b)
             nc.scalar.activation(pa[:], h2[:].indirect(n3_l[:]), COPY)
             ra = keep.tile([P, W], F32, name="ra%d" % b)

@@ -118,7 +118,10 @@ def tile_picked_mthzntsndsubcphw_none_p_kernel(
 
         def scatter_h(t, bank, lo, hi):
             h = keep.tile([P, hi - lo], F32, name="h%d_%d" % (t, lo))
-            nc.vector.tensor_scalar(h[:], bank[:, 0 : hi - lo], gain[:, t : t + 1], None, ALU.mult)
+            if t == 0 and lo == 0:
+                nc.scalar.activation(h[:], bank[:, 0 : hi - lo], COPY, scale=gain[:, t : t + 1])
+            else:
+                nc.vector.tensor_scalar(h[:], bank[:, 0 : hi - lo], gain[:, t : t + 1], None, ALU.mult)
             nc.scalar.activation(ds[t][:].indirect(entries(n1_l, lo, hi)), h[:], COPY)
             nc.scalar.activation(ds2[t][:].indirect(entries(n2_l, lo, hi)), h[:], COPY)
 
@@ -185,20 +188,19 @@ def tile_picked_mthzntsndsubcphw_none_p_kernel(
                 stop=(c == 0),
             )
 
-        parts = [(0, W, S), (0, 0, W)] + [(b, 0, S) for b in range(1, N // P)]
+        parts = [(0, 0, W), (0, W, S)] + [(b, 0, S) for b in range(1, N // P)]
         banks = [psum.tile([P, hi - lo], F32, name="bank_out%d" % i) for i, (b, lo, hi) in enumerate(parts)]
         for bank, (b, lo, hi) in zip(banks, parts):
             second_product(b, bank, 1, two_w, placed3, lo, hi)
 
         last = PACK - 1
-        z_last = keep.tile([P, S], BF16, name="z_last")
-        nc.vector.tensor_tensor(z_last[:, 0:W], ds[last][:, 0:W], ds2[last][:, 0:W], ALU.subtract)
-        nc.vector.tensor_tensor(z_last[:, W:S], ds[last][:, W:S], ds2[last][:, W:S], ALU.subtract)
-        nc.scalar.copy(z[:, 0:W, last], z_last[:, 0:W])
-        nc.vector.tensor_copy(z[:, W:S, last], z_last[:, W:S])
+        z_last = keep.tile([P, W], BF16, name="z_last")
+        nc.vector.tensor_tensor(z_last[:], ds[last][:, 0:W], ds2[last][:, 0:W], ALU.subtract)
+        nc.scalar.copy(z[:, 0:W, last], z_last[:])
+        nc.vector.tensor_tensor(z[:, W:S, last], ds[last][:, W:S], ds2[last][:, W:S], ALU.subtract)
         z_codes = keep.tile([P, S], U32, name="z_codes", align_bytes=64)
         z_scales = keep.tile([P, S], U8, name="z_scales", align_bytes=64)
-        for lo, hi in ((W, S), (0, W)):
+        for lo, hi in ((0, W), (W, S)):
             nc.vector.quantize_mx(
                 out=z_codes[:, lo:hi].bitcast(FP8X4),
                 scales=z_scales[:, lo:hi],
@@ -223,7 +225,7 @@ def tile_picked_mthzntsndsubcphw_none_p_kernel(
             nc.scalar.activation(ub[:].indirect(n6_l[:]), pa[:], COPY)
             nc.scalar.activation(ub[:].indirect(n5_l[:]), ra[:], COPY)
             other = keep.tile([P, S], F32, name="other%d" % b, tag="ra%d" % b)
-            for lo, hi in ((0, REST), (REST, S)):
+            for lo, hi in ((0, W), (W, REST), (REST, S)) if b == N // P - 1 else ((0, W), (W, S)):
                 nc.scalar.activation(other[:, lo:hi], h2[:].indirect(entries(n7_l, lo, hi)), COPY)
                 res = keep.tile([P, hi - lo], F32, name="res%d_%d" % (b, lo))
                 nc.vector.tensor_tensor(res[:], ub[:, lo:hi], other[:, lo:hi], ALU.max)

from contextlib import ExitStack

import concourse.mybir as mybir

K, T, S, N, G, H, W = 512, 1024, 512, 512, 2048, 512, 256
FLOPS = 2 * (2 * K * H * S + H * N * S + K * N * S)

F32 = mybir.dt.float32
BF16 = mybir.dt.bfloat16
I32 = mybir.dt.int32
U32 = mybir.dt.uint32
U16 = mybir.dt.uint16
U8 = mybir.dt.uint8
FP8X4 = mybir.dt.float8_e4m3fn_x4
FP4X4 = mybir.dt.float4_e2m1fn_x4
COPY = mybir.ActivationFunctionType.Copy
ALU = mybir.AluOpType

P = 128
PACK = 4
STRIPE = 16
FIRST = 128
REST = S - FIRST


def tile_picked_mthzntsndsubcphw_none_p_kernel(
    tc, x_words, x_scales, d_words, d_scales, gn, w1_words, w1_scales, w2_words, w2_scales,
    offs, k1, hz, k2, n1, n2, two, n3, n4, n5, n6, n7, out,
):
    nc = tc.nc
    with ExitStack() as ctx:
        lists = ctx.enter_context(tc.tile_pool(name="lists", bufs=1))
        keep = ctx.enter_context(tc.tile_pool(name="keep", bufs=1))
        reuse = ctx.enter_context(tc.tile_pool(name="reuse", bufs=1))
        psum = ctx.enter_context(tc.psum_pool(name="psum", bufs=1))

        def load_list(ap, name):
            t = lists.tile([P, ap.shape[1]], U16, name=name)
            nc.sync.dma_start(t[:], ap)
            return t

        def entries(lst, lo, hi):
            return lst[:, lo // STRIPE : hi // STRIPE]

        def load_scale_table(ap, cols, name):
            t = keep.tile([P, cols], U8, name=name, align_bytes=64)
            rows = ap[0].bitcast(I32)
            nc.scalar.dma_start(t[:].bitcast(I32), rows.unsqueeze(1).to_broadcast([16, 8, cols // 4]))
            return t

        def load_word_table(ap, cols, name):
            t = keep.tile([P, cols], I32, name=name, align_bytes=64)
            nc.gpsimd.dma_start(t[:], ap[0].rearrange("p n t -> p (n t)").bitcast(I32))
            return t

        def place_scale_rows(dst, src, queues):
            for a in range(4):
                q = queues[a % len(queues)]
                q.dma_start(dst[a:P:32, :].bitcast(I32), src[8 * a : P : 32, :].bitcast(I32))

        x_sc = load_scale_table(x_scales, T, "x_sc")
        offs_l = load_list(offs, "offs_l")
        hz_l = load_list(hz, "hz_l")
        d_sc = load_scale_table(d_scales, G, "d_sc")
        k1_l = load_list(k1, "k1_l")
        k2_l = load_list(k2, "k2_l")
        d_w = load_word_table(d_words, G, "d_w")
        x_w = load_word_table(x_words, T, "x_w")
        gain_raw = keep.tile([P, PACK], F32, name="gain_raw")
        nc.sync.dma_start(gain_raw[:], gn.rearrange("(p t) o -> p (t o)", t=PACK))
        n1_l = load_list(n1, "n1_l")
        n2_l = load_list(n2, "n2_l")
        gain = keep.tile([P, PACK], F32, name="gain")
        nc.scalar.activation(gain[:], gain_raw[:], COPY, scale=0.0625)

        def gather(dst, table, dtype, lst, lo, hi):
            nc.vector.tensor_copy(dst, table[:].bitcast(dtype).indirect(entries(lst, lo, hi)) if dtype is U32 else table[:].indirect(entries(lst, lo, hi)))

        placed1 = keep.tile([P, 2 * H + 2 * FIRST], U8, name="placed1", align_bytes=64)
        placed2 = keep.tile([P, 2 * REST], U8, name="placed2", align_bytes=64)
        placed3 = keep.tile([P, S], U8, name="placed3", align_bytes=64)
        nc.vector.memset(placed1[:].bitcast(I32), 0)
        nc.vector.memset(placed2[:].bitcast(I32), 0)
        nc.vector.memset(placed3[:].bitcast(I32), 0)

        picked = reuse.tile([P, 2 * H + 2 * FIRST], U8, name="picked", align_bytes=64, offset=0)
        gather(picked[:, 2 * H : 2 * H + FIRST], x_sc, U8, offs_l, 0, FIRST)
        gather(picked[:, 2 * H + FIRST :], x_sc, U8, hz_l, 0, FIRST)
        gather(picked[:, 0:H], d_sc, U8, k1_l, 0, H)
        gather(picked[:, H : 2 * H], d_sc, U8, k2_l, 0, H)
        place_scale_rows(placed1, picked, (nc.sync, nc.scalar))

        code_w = reuse.tile([P, 2 * H], U32, name="code_w", align_bytes=64, offset=4096)
        gather(code_w[:, 0:H], d_w, U32, k1_l, 0, H)
        gather(code_w[:, H:], d_w, U32, k2_l, 0, H)
        tok_first = keep.tile([P, 2, FIRST], U32, name="tok_first", align_bytes=64)
        gather(tok_first[:, 0, :], x_w, U32, offs_l, 0, FIRST)
        gather(tok_first[:, 1, :], x_w, U32, hz_l, 0, FIRST)

        ds = [keep.tile([P, S], F32, name="ds%d" % t) for t in range(PACK)]
        ds2 = [keep.tile([P, S], F32, name="ds2_%d" % t) for t in range(PACK)]
        dealt_first = keep.tile([P, 2, P], U32, name="dealt_first", align_bytes=64)
        dealt_later = reuse.tile([P, PACK - 1, 2, P], U32, name="dealt_later", align_bytes=64, offset=0)
        dealt_w = [dealt_first[:]] + [dealt_later[:, t] for t in range(PACK - 1)]
        dealt_s = [keep.tile([P, 2, P], U8, name="dealt_s%d" % t, align_bytes=64) for t in range(PACK)]

        def first_product(t, bank, tok, tok_scale, lo, hi, base):
            for c in range(2):
                nc.tensor.matmul_mx(
                    out=bank[:, lo - base : hi - base],
                    lhsT=dealt_w[t][:, c, :].bitcast(FP8X4),
                    lhsT_scale=dealt_s[t][:, c, :],
                    rhs=tok[:, c, lo - base : hi - base].bitcast(FP8X4),
                    rhs_scale=tok_scale[:, c, lo - base : hi - base],
                    start=(c == 0),
                    stop=(c == 1),
                )

        def scatter_h(t, bank, lo, hi):
            h = keep.tile([P, hi - lo], F32, name="h%d_%d" % (t, lo))
            if t == 0 and lo == 0:
                nc.scalar.activation(h[:], bank[:, 0 : hi - lo], COPY, scale=gain[:, t : t + 1])
            else:
                nc.vector.tensor_scalar(h[:], bank[:, 0 : hi - lo], gain[:, t : t + 1], None, ALU.mult)
            nc.scalar.activation(ds[t][:].indirect(entries(n1_l, lo, hi)), h[:], COPY)
            nc.scalar.activation(ds2[t][:].indirect(entries(n2_l, lo, hi)), h[:], COPY)

        first_scale = placed1[:, 2 * H :].rearrange("p (c n) -> p c n", c=2)
        for t in range(PACK):
            nc.vector.tensor_copy(
                dealt_w[t].bitcast(I32),
                code_w[:].bitcast(I32).rearrange("p (c m t) -> p t c m", c=2, t=PACK)[:, t],
            )
            nc.vector.tensor_copy(
                dealt_s[t][:], placed1[:, 0 : 2 * H].rearrange("p (c m t) -> p t c m", c=2, t=PACK)[:, t]
            )
            bank = psum.tile([P, FIRST], F32, name="bank_first%d" % t, tag="bank_out%d" % t)
            first_product(t, bank, tok_first, first_scale, 0, FIRST, 0)
            scatter_h(t, bank, 0, FIRST)

        picked_rest = reuse.tile([P, 2 * REST], U8, name="picked_rest", align_bytes=64, offset=4096 + 8 * REST)
        gather(picked_rest[:, 0:REST], x_sc, U8, offs_l, FIRST, S)
        gather(picked_rest[:, REST:], x_sc, U8, hz_l, FIRST, S)
        place_scale_rows(placed2, picked_rest, (nc.sync,))

        tok_rest = reuse.tile([P, 2, REST], U32, name="tok_rest", align_bytes=64, offset=4096)
        gather(tok_rest[:, 0, :], x_w, U32, offs_l, FIRST, S)
        gather(tok_rest[:, 1, :], x_w, U32, hz_l, FIRST, S)
        rest_scale = placed2[:].rearrange("p (c n) -> p c n", c=2)

        two_l = load_list(two, "two_l")
        n3_l = load_list(n3, "n3_l")
        n4_l = load_list(n4, "n4_l")
        n5_l = load_list(n5, "n5_l")
        n6_l = load_list(n6, "n6_l")
        n7_l = load_list(n7, "n7_l")
        w_codes = keep.tile([P, 2, 2 * N], U8, name="w_codes", tag="d_w", align_bytes=64)
        w_sc = keep.tile([P, 2, N], U8, name="w_sc", tag="placed1", align_bytes=64)
        nc.gpsimd.memset(w_sc[:].rearrange("p a n -> p (a n)").bitcast(I32), 0)
        for c, (words, scales) in enumerate(((w1_words, w1_scales), (w2_words, w2_scales))):
            nc.sync.dma_start(w_codes[:, c, :].bitcast(I32), words[0].bitcast(I32))
            for a in range(4):
                nc.sync.dma_start(w_sc[a:P:32, c, :].bitcast(I32), scales[0, a:16:4, :].bitcast(I32))

        z = keep.tile([P, S, PACK], BF16, name="z", align_bytes=64)
        for t in range(PACK):
            bank = psum.tile([P, REST], F32, name="bank_rest", bufs=2)
            first_product(t, bank, tok_rest, rest_scale, FIRST, FIRST + 256, FIRST)
            first_product(t, bank, tok_rest, rest_scale, FIRST + 256, S, FIRST)
            scatter_h(t, bank, FIRST, S)
            if t < PACK - 1:
                nc.vector.tensor_tensor(z[:, :, t], ds[t][:], ds2[t][:], ALU.subtract)

        picked_two = reuse.tile([P, S], U8, name="picked_two", align_bytes=64, offset=0)
        gather(picked_two[:], x_sc, U8, two_l, 0, S)
        place_scale_rows(placed3, picked_two, (nc.sync,))
        two_w = reuse.tile([P, S], U32, name="two_w", align_bytes=64, offset=4096)
        gather(two_w[:], x_w, U32, two_l, 0, S)

        def second_product(b, bank, c, rhs, rhs_scale, lo, hi):
            nc.tensor.matmul_mx(
                out=bank[:],
                lhsT=w_codes[:, c, 2 * P * b : 2 * P * (b + 1)].bitcast(FP4X4),
                lhsT_scale=w_sc[:, c, P * b : P * (b + 1)],
                rhs=rhs[:, lo:hi].bitcast(FP8X4),
                rhs_scale=rhs_scale[:, lo:hi],
                start=(c == 1),
                stop=(c == 0),
            )

        parts = [(0, 0, W), (0, W, S)] + [(b, 0, S) for b in range(1, N // P)]
        banks = [psum.tile([P, hi - lo], F32, name="bank_out%d" % i) for i, (b, lo, hi) in enumerate(parts)]
        for bank, (b, lo, hi) in zip(banks, parts):
            second_product(b, bank, 1, two_w, placed3, lo, hi)

        last = PACK - 1
        z_last = keep.tile([P, W], BF16, name="z_last")
        nc.vector.tensor_tensor(z_last[:], ds[last][:, 0:W], ds2[last][:, 0:W], ALU.subtract)
        nc.scalar.copy(z[:, 0:W, last], z_last[:])
        nc.vector.tensor_tensor(z[:, W:S, last], ds[last][:, W:S], ds2[last][:, W:S], ALU.subtract)
        z_codes = keep.tile([P, S], U32, name="z_codes", align_bytes=64)
        z_scales = keep.tile([P, S], U8, name="z_scales", align_bytes=64)
        for lo, hi in ((0, W), (W, S)):
            nc.vector.quantize_mx(
                out=z_codes[:, lo:hi].bitcast(FP8X4),
                scales=z_scales[:, lo:hi],
                in_=z[:, lo:hi, :].rearrange("p n t -> p (n t)"),
            )

        h2s = [keep.tile([P, S], F32, name="h2_%d" % b) for b in range(N // P)]
        for bank, (b, lo, hi) in zip(banks, parts):
            second_product(b, bank, 0, z_codes, z_scales, lo, hi)
            if b == 0:
                nc.scalar.copy(h2s[b][:, lo:hi], bank[:])

        for b in range(N // P):
            h2 = h2s[b]
            if b > 0:
                nc.vector.tensor_copy(h2[:], banks[b + 1][:])
            pa = keep.tile([P, W], F32, name="pa%d" % b)
            nc.scalar.activation(pa[:], h2[:].indirect(n3_l[:]), COPY)
            ra = keep.tile([P, W], F32, name="ra%d" % b)
            nc.vector.tensor_tensor(ra[:], h2[:].indirect(n4_l[:]), pa[:], ALU.subtract)
            ub = keep.tile([P, S], F32, name="ub%d" % b)
            nc.scalar.activation(ub[:].indirect(n6_l[:]), pa[:], COPY)
            nc.scalar.activation(ub[:].indirect(n5_l[:]), ra[:], COPY)
            other = keep.tile([P, S], F32, name="other%d" % b, tag="ra%d" % b)
            for lo, hi in ((0, W), (W, REST), (REST, S)) if b == N // P - 1 else ((0, W), (W, S)):
                nc.scalar.activation(other[:, lo:hi], h2[:].indirect(entries(n7_l, lo, hi)), COPY)
                res = keep.tile([P, hi - lo], F32, name="res%d_%d" % (b, lo))
                nc.vector.tensor_tensor(res[:], ub[:, lo:hi], other[:, lo:hi], ALU.max)
                nc.sync.dma_start(out[P * b : P * (b + 1), lo:hi], res[:])
